import numpy as np
import ml_dtypes


def mxq(x, axis, fmt="e4m3"):
    dtype, down = {"e4m3": (ml_dtypes.float8_e4m3fn, 7), "e5m2": (ml_dtypes.float8_e5m2, 14)}[fmt]
    v = np.moveaxis(np.asarray(x, np.float32).astype(ml_dtypes.bfloat16).astype(np.float64), axis, -1)
    blocks = v.reshape(v.shape[:-1] + (-1, 32))
    amax = np.abs(blocks).max(-1, keepdims=True)
    byte = np.maximum(np.where(amax > 0, np.frexp(amax)[1] - 1 + 127, 0) - down, 1)
    scale = np.exp2(byte - 127.0)
    codes = (blocks / scale).astype(np.float32).astype(dtype).astype(np.float64)
    return np.moveaxis((codes * scale).reshape(v.shape), -1, axis)


WIDE = False


def mx_kscale(k):
    if not WIDE:
        return np.ones(k)
    levels = np.array([10, -10, 5, -5, 0])
    if k % 512:
        return np.exp2(np.random.permutation(np.resize(levels, k // 32))).repeat(32)
    a = np.empty((k // 512, 16))
    for p in range(k // 512):
        a[p, :8] = np.random.permutation(np.resize(levels, 8))
        for g in range(8):
            far = levels[np.abs(levels - a[p, g]) >= 10]
            a[p, g + 8] = far[np.random.randint(len(far))]
    return np.exp2(a.ravel()).repeat(32)


def f64(x):
    return np.asarray(x).astype(np.float64)


def striped(idx):
    return np.tile(idx.reshape(-1, 16).T, (8, 1)).astype(np.uint16)


def unstriped(offs):
    return offs[:16].T.reshape(-1).astype(np.int64)


E2M1 = np.array([0.0, 0.5, 1.0, 1.5, 2.0, 3.0, 4.0, 6.0, -0.0, -0.5, -1.0, -1.5, -2.0, -3.0, -4.0, -6.0])


def pack_weight(w, fmt):
    k, n = w.shape
    w = f64(np.asarray(w, np.float32).astype(ml_dtypes.bfloat16)).reshape(k // 32, 32, n)
    amax = np.abs(w).max(1)
    if fmt == "e4m3":
        byte = np.frexp(amax)[1] - 1 + 127 - 7
    else:
        mant, ex = np.frexp(amax / 6.0)
        byte = np.where(mant > 0.5, ex, ex - 1) + 127
    byte = np.clip(np.where(amax > 0, byte, 1), 1, 254)
    scaled = (w * np.exp2(127.0 - byte)[:, None, :]).reshape(k, n).astype(np.float32)
    by_word = np.ascontiguousarray(scaled.reshape(k // 512, 128, 4, n).transpose(0, 1, 3, 2))
    if fmt == "e4m3":
        words = by_word.astype(ml_dtypes.float8_e4m3fn).view(np.uint8)
    else:
        c = by_word.astype(ml_dtypes.float4_e2m1fn).view(np.uint8) & 0xF
        words = (c[..., 0::2] | (c[..., 1::2] << 4)).reshape(k // 512, 128, 2 * n)
    return np.ascontiguousarray(words), np.ascontiguousarray(byte.astype(np.uint8).reshape(k // 512, 16, n))


def unpack_weight(words, scales, fmt):
    g, _, n = scales.shape
    words = np.ascontiguousarray(words).reshape(g, 128, n, -1)
    if fmt == "e4m3":
        vals = words.view(ml_dtypes.float8_e4m3fn).astype(np.float64)
    else:
        nib = np.empty((g, 128, n, 4), np.uint8)
        nib[..., 0::2] = words & 0xF
        nib[..., 1::2] = words >> 4
        vals = E2M1[nib]
    vals = vals * np.repeat(np.exp2(scales.astype(np.float64) - 127.0), 8, axis=1)[..., None]
    return vals.transpose(0, 1, 3, 2).reshape(g * 512, n)


def gelu(v):
    return 0.5 * v * (1.0 + np.tanh(np.sqrt(2.0 / np.pi) * (v + 0.044715 * v**3)))


K, T, S, H, P, N = 512, 4096, 1024, 1024, 512, 384


def setup_inputs():
    n = np.random.standard_normal
    s = mx_kscale(K)[:, None]
    u = mx_kscale(H)[:, None]
    d = {}
    d["tab_words"], d["tab_scales"] = pack_weight(n((K, T)) * s, "e2m1")
    d["offs"] = striped(np.random.permutation(T)[:S])
    d["pos1"] = striped(np.random.permutation(S)[:P])
    d["pos2"] = striped(np.random.permutation(S)[:P])
    d["wa"] = (n((K, H)) / K ** 0.5 / s * u.T).astype(np.float32)
    d["wb"] = (n((K, H)) / K ** 0.5 / s * u.T).astype(np.float32)
    d["wd_words"], d["wd_scales"] = pack_weight(n((K, H)) / K ** 0.5 / s * u.T, "e4m3")
    d["bd"] = ((0.8 + 0.5 * n(H)) * u[:, 0]).astype(np.float32)
    d["w4_words"], d["w4_scales"] = pack_weight(1.3 * n((H, N)) / H ** 0.5 / u, "e2m1")
    d["b4"] = (0.5 * n(N)).astype(np.float32)
    return d


def reference(tab_words, tab_scales, offs, pos1, pos2, wa, wb, wd_words, wd_scales, bd, w4_words, w4_scales, b4):
    v = unpack_weight(tab_words, tab_scales, "e2m1")[:, unstriped(offs)]
    wd = unpack_weight(wd_words, wd_scales, "e4m3")
    w4 = unpack_weight(w4_words, w4_scales, "e2m1")
    a = mxq(f64(wa), 0, "e4m3").T @ v
    b = mxq(f64(wb), 0, "e4m3").T @ v
    e = (wd.T @ v) + f64(bd)[:, None]
    h = np.minimum(np.maximum(a, b), e)
    x = h[:, unstriped(pos1)] - h[:, unstriped(pos2)]
    y = w4.T @ mxq(x, 0, "e4m3")
    return np.tanh(y + f64(b4)[:, None])

@@ -1,0 +1,301 @@
+from contextlib import ExitStack
+
+import concourse.mybir as mybir
+
+K, T, S, H, M, N = 512, 4096, 1024, 1024, 512, 384
+FLOPS = 3 * 2 * K * H * S + 2 * H * N * M
+
+F32 = mybir.dt.float32
+BF16 = mybir.dt.bfloat16
+I32 = mybir.dt.int32
+U32 = mybir.dt.uint32
+U16 = mybir.dt.uint16
+U8 = mybir.dt.uint8
+FP8X4 = mybir.dt.float8_e4m3fn_x4
+FP4X4 = mybir.dt.float4_e2m1fn_x4
+ALU = mybir.AluOpType
+ACT = mybir.ActivationFunctionType
+
+P = 128
+PACK = 4
+PASS = P * PACK
+BANK = 512
+LOAD_COLS = 256
+UNIT = 128
+
+
+def tile_list_clamped_pair_features_kernel(
+    tc, tab_words, tab_scales, offs, pos1, pos2, wa, wb, wd_words, wd_scales, bd, w4_words, w4_scales, b4, out
+):
+    nc = tc.nc
+    with ExitStack() as ctx:
+        keep = ctx.enter_context(tc.tile_pool(name="keep", bufs=1))
+        ring = ctx.enter_context(tc.tile_pool(name="ring", bufs=3))
+        psum = ctx.enter_context(tc.psum_pool(name="psum", bufs=1))
+
+        offs_sb = keep.tile([P, S // 16], U16, name="offs_sb")
+        pos1_sb = keep.tile([P, M // 16], U16, name="pos1_sb")
+        pos2_sb = keep.tile([P, M // 16], U16, name="pos2_sb")
+        nc.sync.dma_start(offs_sb[:], offs)
+
+        tab_bytes = keep.tile([P, T], U8, name="tab_bytes")
+        nc.sync.dma_start(tab_bytes[112:128, :].bitcast(I32), tab_scales[0].bitcast(I32))
+        nc.vector.memset(tab_bytes[0:112, :].bitcast(I32), 0)
+        nc.sync.dma_start(pos1_sb[:], pos1)
+        nc.sync.dma_start(pos2_sb[:], pos2)
+        bd_sb = keep.tile([P, 2, PACK], F32, name="bd_sb")
+        nc.sync.dma_start(bd_sb[:], bd.rearrange("(b p t) -> p b t", b=2, t=PACK))
+
+        tab_sb = keep.tile([P, T], U16, name="tab_sb")
+        nc.sync.dma_start(tab_sb[:].bitcast(I32), tab_words[0].bitcast(I32))
+
+        def load_weight(w, which, b, c):
+            raw = keep.tile([P, PACK, LOAD_COLS], F32, name="raw_%s%d%d" % (which, b, c), tag="slot_%s%d" % (which, c), align_bytes=64)
+            c0 = PASS * b + LOAD_COLS * c
+            nc.sync.dma_start(raw[:], w.rearrange("(p j) r -> p j r", j=PACK)[:, :, c0 : c0 + LOAD_COLS])
+            return raw
+
+        def round_weight(copy, raw, grouped, c):
+            q0, nq = c * LOAD_COLS // PACK, LOAD_COLS // PACK
+            copy(
+                grouped[:, :, q0 : q0 + nq, :].rearrange("p t q j -> p q t j"),
+                raw[:].rearrange("p j (q t) -> p q t j", t=PACK),
+            )
+
+        def quantize(name, grouped_flat, widths):
+            words = grouped_flat.shape[1] // PACK
+            codes = keep.tile([P, words], U32, name=name + "_codes", align_bytes=64)
+            scales = keep.tile([P, words], U8, name=name + "_scales", align_bytes=64)
+            w0 = 0
+            for width in widths:
+                nc.vector.quantize_mx(
+                    out=codes[:, w0 : w0 + width].bitcast(FP8X4),
+                    scales=scales[:, w0 : w0 + width],
+                    in_=grouped_flat[:, PACK * w0 : PACK * (w0 + width)],
+                )
+                w0 = w0 + width
+            return codes, scales
+
+        def load_scale_rows(queue, dst, src):
+            for r in range(4):
+                queue.dma_start(dst[r:P:32, :, :].bitcast(I32), src[r:16:4, :, :].bitcast(I32))
+
+        raw_a = [load_weight(wa, "a", 0, c) for c in range(2)]
+        raw_b = [load_weight(wb, "b", 0, c) for c in range(2)]
+
+        v_scales = keep.tile([P, S], U8, name="v_scales", align_bytes=64)
+        wd_bytes = keep.tile([P, H], U8, name="wd_bytes", tag="slot_scales", align_bytes=64)
+        warm = keep.tile([P, 2], F32, name="warm")
+        nc.gpsimd.memset(warm[:, 0:1], 0.0)
+        nc.scalar.activation(warm[:, 1:2], warm[:, 0:1], ACT.Tanh)
+        nc.gpsimd.memset(wd_bytes[:].bitcast(I32), 0)
+        nc.vector.memset(v_scales[:].bitcast(I32), 0)
+        load_scale_rows(nc.gpsimd, wd_bytes[:].rearrange("p (a n) -> p a n", a=1), wd_scales.rearrange("a q n -> q a n"))
+
+        picked_bytes = keep.tile([P, S], U8, name="picked_bytes", tag="slot_picked")
+        nc.vector.tensor_copy(picked_bytes[:], tab_bytes[:].indirect(offs_sb[:]))
+        for quad in range(4):
+            nc.scalar.dma_start(
+                v_scales[32 * quad : 32 * quad + 4, :].bitcast(I32),
+                picked_bytes[112 + 4 * quad : 116 + 4 * quad, :].bitcast(I32),
+            )
+
+        b4_sb = keep.tile([P, N // P], F32, name="b4_sb", tag="slot_picked")
+        with nc.allow_non_contiguous_dma(reason="one bias value a partition"):
+            nc.sync.dma_start(b4_sb[:], b4.rearrange("(c p) -> p c", p=P))
+
+        v_words = keep.tile([P, S], U16, name="v_words", align_bytes=64)
+        nc.vector.tensor_copy(v_words[:], tab_sb[:].indirect(offs_sb[:]))
+
+        def load_wd(b):
+            raw = keep.tile([P, PASS], I32, name="raw_d%d" % b, tag="slot_d%d" % b, align_bytes=64)
+            flat = wd_words[0].rearrange("p r i -> p (r i)")
+            nc.sync.dma_start(raw[:], flat[:, PACK * PASS * b : PACK * PASS * (b + 1)].bitcast(I32))
+            return raw
+
+        def deal_wd(raw, b):
+            codes = keep.tile([P, PASS], I32, name="wd_codes%d" % b, align_bytes=64)
+            scales = keep.tile([P, PASS], U8, name="wd_scales%d" % b, align_bytes=64)
+            nc.vector.tensor_copy(
+                codes[:].rearrange("p (t g i) -> p g t i", t=PACK, i=4),
+                raw[:].rearrange("p (g i t) -> p g t i", t=PACK, i=4),
+            )
+            nc.vector.tensor_copy(
+                scales[:].rearrange("p (t g i) -> p g t i", t=PACK, i=16),
+                wd_bytes[:, PASS * b : PASS * (b + 1)].rearrange("p (g i t) -> p g t i", t=PACK, i=16),
+            )
+            return codes, scales
+
+        def grouped_tile(name, tag):
+            return keep.tile([P, PACK, P, PACK], BF16, name=name, tag=tag, align_bytes=64)
+
+        def flat(grouped):
+            return grouped[:].rearrange("p t q j -> p (t q j)")
+
+        raw_d = load_wd(0)
+        ga, gb = grouped_tile("ga0", "slot_ga"), grouped_tile("gb0", "slot_d1")
+        round_weight(nc.scalar.copy, raw_a[0], ga, 0)
+        round_weight(nc.scalar.copy, raw_a[1], ga, 1)
+        round_weight(nc.vector.tensor_copy, raw_b[0], gb, 0)
+        qa = [quantize("wa0", flat(ga), [512])]
+        round_weight(nc.vector.tensor_copy, raw_b[1], gb, 1)
+        qd = [deal_wd(raw_d, 0)]
+        qb = [quantize("wb0", flat(gb), [128, 128, 256])]
+
+        raw_a = [load_weight(wa, "a", 1, c) for c in range(2)]
+        raw_b = [load_weight(wb, "b", 1, c) for c in range(2)]
+        raw_d = load_wd(1)
+        ga, gb = grouped_tile("ga1", "slot_ga"), grouped_tile("gb1", "slot_gb")
+
+        h = [keep.tile([P, S], F32, name="h%d" % i) for i in range(H // P)]
+
+        def product(tag, bufs, operand, t, half):
+            codes, scales = operand
+            acc = psum.tile([P, BANK], F32, name=tag, tag=tag, bufs=bufs)
+            cols = slice(BANK * half, BANK * (half + 1))
+            nc.tensor.matmul_mx(
+                out=acc[:],
+                lhsT=codes[:, P * t : P * (t + 1)].bitcast(FP8X4),
+                lhsT_scale=scales[:, P * t : P * (t + 1)],
+                rhs=v_words[:, cols].bitcast(FP4X4),
+                rhs_scale=v_scales[:, cols],
+                start=True,
+                stop=True,
+            )
+            return acc
+
+        def products(b, t, half):
+            a_ps = product("ps_a", 2, qa[b], t, half)
+            b_ps = product("ps_b", 3, qb[b], t, half)
+            e_ps = product("ps_e", 3, qd[b], t, half)
+            a_sb = ring.tile([P, BANK], F32, name="a_sb")
+            nc.scalar.copy(a_sb[:], a_ps[:])
+            return a_sb, b_ps, e_ps
+
+        def floor(unit):
+            floored = ring.tile([P, BANK], F32, name="floored")
+            nc.vector.tensor_tensor(floored[:], unit[1][:], unit[0][:], ALU.max)
+            return floored
+
+        def ceiling(unit, floored, b, t, half):
+            nc.vector.scalar_tensor_tensor(
+                h[PACK * b + t][:, BANK * half : BANK * (half + 1)],
+                unit[2][:], bd_sb[:, b, t : t + 1], floored[:], ALU.add, ALU.min,
+            )
+
+        def pick_control(i, m0, m1):
+            control = ring.tile([P, m1 - m0], F32, name="control", tag="control")
+            nc.vector.tensor_copy(control[:], h[i][:].indirect(pos2_sb[:, m0 // 16 : m1 // 16]))
+            return control
+
+        def pick_difference(i, control, x32, m0, m1):
+            nc.vector.tensor_tensor(
+                x32[:, i % PACK, :], h[i][:].indirect(pos1_sb[:, m0 // 16 : m1 // 16]), control[:], ALU.subtract
+            )
+
+        def round_x(copy, x32, x16, m0, m1):
+            copy(
+                x16[:, m0:m1, :].rearrange("p (g i) t -> p g t i", i=4),
+                x32[:, :, m0:m1].rearrange("p t (g i) -> p g t i", i=4),
+            )
+
+        def x_tiles(name, width):
+            x32 = keep.tile([P, PACK, width], F32, name=name + "_32")
+            x16 = keep.tile([P, width, PACK], BF16, name=name + "_16", align_bytes=64)
+            return x32, x16
+
+        x0_32, x0_16 = x_tiles("x0", M)
+        chunks = [(0, 256), (256, 384), (384, 512)]
+        x1 = [x_tiles("x1_%d" % c, m1 - m0) for c, (m0, m1) in enumerate(chunks)]
+
+        def inline_picks(i):
+            return (x0_32, 0, M) if i < PACK else (x1[0][0], chunks[0][0], chunks[0][1])
+
+        w4_sb = None
+        w4_scales_sb = None
+        qx0 = None
+        for i in range(H // P):
+            b, t = divmod(i, PACK)
+            units = [products(b, t, half) for half in range(2)]
+            floored0 = floor(units[0])
+            if i > 0:
+                x32, m0, m1 = inline_picks(i - 1)
+                control = pick_control(i - 1, m0, m1)
+            floored1 = floor(units[1])
+            ceiling(units[0], floored0, b, t, 0)
+            if i > 0:
+                pick_difference(i - 1, control, x32, m0, m1)
+            ceiling(units[1], floored1, b, t, 1)
+            if i == 0:
+                round_weight(nc.scalar.copy, raw_a[0], ga, 0)
+                round_weight(nc.scalar.copy, raw_a[1], ga, 1)
+            if i == 1:
+                round_weight(nc.scalar.copy, raw_b[0], gb, 0)
+                round_weight(nc.scalar.copy, raw_b[1], gb, 1)
+                qa.append(quantize("wa1", flat(ga), [512]))
+                qd.append(deal_wd(raw_d, 1))
+                w4_sb = keep.tile([P, 2, 2 * N], U8, name="w4_sb", tag="slot_d1", align_bytes=64)
+                nc.sync.dma_start(w4_sb[:].bitcast(I32), w4_words.rearrange("a p n -> p a n").bitcast(I32))
+                w4_scales_sb = keep.tile([P, 2, N], U8, name="w4_scales_sb", tag="slot_scales", align_bytes=64)
+                nc.gpsimd.memset(w4_scales_sb[:].rearrange("p a n -> p (a n)").bitcast(I32), 0)
+                load_scale_rows(nc.sync, w4_scales_sb[:], w4_scales.rearrange("a q n -> q a n"))
+            if i == 2:
+                qb.append(quantize("wb1", flat(gb), [512]))
+            if i == 4:
+                round_x(nc.scalar.copy, x0_32, x0_16, 0, 256)
+                round_x(nc.scalar.copy, x0_32, x0_16, 256, 512)
+            if i == 5:
+                qx0 = quantize("x0", x0_16[:].rearrange("p m t -> p (m t)"), [512])
+
+        def last_passes(acc, b, operand, c0):
+            codes, scales = operand
+            for n in range(N // P):
+                nc.tensor.matmul_mx(
+                    out=acc[:, UNIT * n : UNIT * (n + 1)],
+                    lhsT=w4_sb[:, b, 2 * P * n : 2 * P * (n + 1)].bitcast(FP4X4),
+                    lhsT_scale=w4_scales_sb[:, b, P * n : P * (n + 1)],
+                    rhs=codes[:, c0 : c0 + UNIT].bitcast(FP8X4),
+                    rhs_scale=scales[:, c0 : c0 + UNIT],
+                    start=(b == 0 and n == 0),
+                    stop=(b == 1 and n == N // P - 1),
+                )
+
+        y_ps = []
+        for u, (tag, bufs) in enumerate([("ps_a", 2), ("ps_a", 2), ("ps_b", 3), ("ps_e", 3)]):
+            acc = psum.tile([P, BANK], F32, name="y%d" % u, tag=tag, bufs=bufs)
+            last_passes(acc, 0, qx0, UNIT * u)
+            y_ps.append(acc)
+
+        def finish(c):
+            m0, m1 = chunks[c]
+            qx = quantize("x1_%d" % c, x1[c][1][:].rearrange("p m t -> p (m t)"), [m1 - m0])
+            for u in range(m0 // UNIT, m1 // UNIT):
+                last_passes(y_ps[u], 1, qx, UNIT * u - m0)
+                result = keep.tile([P, N // P, UNIT], F32, name="result%d" % u)
+                for n in range(N // P):
+                    nc.scalar.activation(
+                        result[:, n, :], y_ps[u][:, UNIT * n : UNIT * (n + 1)], ACT.Tanh, bias=b4_sb[:, n : n + 1]
+                    )
+                nc.sync.dma_start(
+                    out.rearrange("(c p) m -> p c m", p=P)[:, :, UNIT * u : UNIT * (u + 1)], result[:]
+                )
+
+        def picks(c, tiles):
+            m0, m1 = chunks[c]
+            controls = [pick_control(i, m0, m1) for i in tiles]
+            for i, control in zip(tiles, controls):
+                pick_difference(i, control, x1[c][0], m0, m1)
+
+        control4 = pick_control(4, *chunks[1])
+        control7 = pick_control(7, *chunks[0])
+        pick_difference(4, control4, x1[1][0], *chunks[1])
+        pick_difference(7, control7, x1[0][0], *chunks[0])
+        round_x(nc.scalar.copy, x1[0][0], x1[0][1], 0, 256)
+        picks(1, [5, 6, 7])
+        round_x(nc.scalar.copy, x1[1][0], x1[1][1], 0, 128)
+        finish(0)
+        picks(2, [4, 5])
+        finish(1)
+        picks(2, [6, 7])
+        round_x(nc.vector.tensor_copy, x1[2][0], x1[2][1], 0, 128)
+        finish(2)

@@ -115,16 +115,11 @@ def tile_list_clamped_pair_features_kernel(
 
         def deal_wd(raw, b):
             codes = keep.tile([P, PASS], I32, name="wd_codes%d" % b, align_bytes=64)
-            scales = keep.tile([P, PASS], U8, name="wd_scales%d" % b, align_bytes=64)
             nc.vector.tensor_copy(
                 codes[:].rearrange("p (t g i) -> p g t i", t=PACK, i=4),
                 raw[:].rearrange("p (g i t) -> p g t i", t=PACK, i=4),
             )
-            nc.vector.tensor_copy(
-                scales[:].rearrange("p (t g i) -> p g t i", t=PACK, i=16),
-                wd_bytes[:, PASS * b : PASS * (b + 1)].rearrange("p (g i t) -> p g t i", t=PACK, i=16),
-            )
-            return codes, scales
+            return codes, wd_dealt[:, PASS * b : PASS * (b + 1)]
 
         def grouped_tile(name, tag):
             return keep.tile([P, PACK, P, PACK], BF16, name=name, tag=tag, align_bytes=64)
@@ -139,13 +134,18 @@ def tile_list_clamped_pair_features_kernel(
         round_weight(nc.vector.tensor_copy, raw_b[0], gb, 0)
         qa = [quantize("wa0", flat(ga), [512])]
         round_weight(nc.vector.tensor_copy, raw_b[1], gb, 1)
+        wd_dealt = keep.tile([P, H], U8, name="wd_dealt", tag="slot_ga", align_bytes=64)
+        nc.vector.tensor_copy(
+            wd_dealt[:].rearrange("p (b t g i) -> p b g t i", b=2, t=PACK, i=16),
+            wd_bytes[:].rearrange("p (b g i t) -> p b g t i", b=2, t=PACK, i=16),
+        )
         qd = [deal_wd(raw_d, 0)]
         qb = [quantize("wb0", flat(gb), [128, 128, 256])]
 
         raw_a = [load_weight(wa, "a", 1, c) for c in range(2)]
         raw_b = [load_weight(wb, "b", 1, c) for c in range(2)]
         raw_d = load_wd(1)
-        ga, gb = grouped_tile("ga1", "slot_ga"), grouped_tile("gb1", "slot_gb")
+        ga, gb = grouped_tile("ga1", "slot_ga1"), grouped_tile("gb1", "slot_gb")
 
         h = [keep.tile([P, S], F32, name="h%d" % i) for i in range(H // P)]
 
@@ -172,8 +172,9 @@ def tile_list_clamped_pair_features_kernel(
             nc.scalar.copy(a_sb[:], a_ps[:])
             return a_sb, b_ps, e_ps
 
-        def floor(unit):
-            floored = ring.tile([P, BANK], F32, name="floored")
+        def floor(unit, floored=None):
+            if floored is None:
+                floored = ring.tile([P, BANK], F32, name="floored")
             nc.vector.tensor_tensor(floored[:], unit[1][:], unit[0][:], ALU.max)
             return floored
 
@@ -183,14 +184,14 @@ def tile_list_clamped_pair_features_kernel(
                 unit[2][:], bd_sb[:, b, t : t + 1], floored[:], ALU.add, ALU.min,
             )
 
-        def pick_control(i, m0, m1):
-            control = ring.tile([P, m1 - m0], F32, name="control", tag="control")
-            nc.vector.tensor_copy(control[:], h[i][:].indirect(pos2_sb[:, m0 // 16 : m1 // 16]))
+        def pick_control(i):
+            control = keep.tile([P, M], F32, name="control%d" % i, tag="control%d" % (i % PACK))
+            nc.vector.tensor_copy(control[:], h[i][:].indirect(pos2_sb[:]))
             return control
 
-        def pick_difference(i, control, x32, m0, m1):
+        def pick_difference(i, x32, m0, m1):
             nc.vector.tensor_tensor(
-                x32[:, i % PACK, :], h[i][:].indirect(pos1_sb[:, m0 // 16 : m1 // 16]), control[:], ALU.subtract
+                x32[:, i % PACK, :], h[i][:].indirect(pos1_sb[:, m0 // 16 : m1 // 16]), controls[i][:, m0:m1], ALU.subtract
             )
 
         def round_x(copy, x32, x16, m0, m1):
@@ -199,14 +200,15 @@ def tile_list_clamped_pair_features_kernel(
                 x32[:, :, m0:m1].rearrange("p t (g i) -> p g t i", i=4),
             )
 
-        def x_tiles(name, width):
-            x32 = keep.tile([P, PACK, width], F32, name=name + "_32")
-            x16 = keep.tile([P, width, PACK], BF16, name=name + "_16", align_bytes=64)
+        def x_tiles(name, width, tag32, tag16):
+            x32 = keep.tile([P, PACK, width], F32, name=name + "_32", tag=tag32, align_bytes=64)
+            x16 = keep.tile([P, width, PACK], BF16, name=name + "_16", tag=tag16, align_bytes=64)
             return x32, x16
 
-        x0_32, x0_16 = x_tiles("x0", M)
+        x0_32, x0_16 = x_tiles("x0", M, "x0_32", "x0_16")
         chunks = [(0, 256), (256, 384), (384, 512)]
-        x1 = [x_tiles("x1_%d" % c, m1 - m0) for c, (m0, m1) in enumerate(chunks)]
+        x1 = [x_tiles("x1_%d" % c, chunks[c][1] - chunks[c][0], "x1_32_%d" % c, "x1_16_%d" % c) for c in range(1)]
+        controls = []
 
         def inline_picks(i):
             return (x0_32, 0, M) if i < PACK else (x1[0][0], chunks[0][0], chunks[0][1])
@@ -219,12 +221,12 @@ def tile_list_clamped_pair_features_kernel(
             units = [products(b, t, half) for half in range(2)]
             floored0 = floor(units[0])
             if i > 0:
-                x32, m0, m1 = inline_picks(i - 1)
-                control = pick_control(i - 1, m0, m1)
-            floored1 = floor(units[1])
+                controls.append(pick_control(i - 1))
+            last = keep.tile([P, BANK], F32, name="last", tag="x1_32_1", align_bytes=64) if i == 7 else None
+            floored1 = floor(units[1], last)
             ceiling(units[0], floored0, b, t, 0)
             if i > 0:
-                pick_difference(i - 1, control, x32, m0, m1)
+                pick_difference(i - 1, *inline_picks(i - 1))
             ceiling(units[1], floored1, b, t, 1)
             if i == 0:
                 round_weight(nc.scalar.copy, raw_a[0], ga, 0)
@@ -276,26 +278,20 @@ def tile_list_clamped_pair_features_kernel(
                     nc.scalar.activation(
                         result[:, n, :], y_ps[u][:, UNIT * n : UNIT * (n + 1)], ACT.Tanh, bias=b4_sb[:, n : n + 1]
                     )
-                nc.sync.dma_start(
-                    out.rearrange("(c p) m -> p c m", p=P)[:, :, UNIT * u : UNIT * (u + 1)], result[:]
-                )
+                    nc.sync.dma_start(out[P * n : P * (n + 1), UNIT * u : UNIT * (u + 1)], result[:, n, :])
 
-        def picks(c, tiles):
-            m0, m1 = chunks[c]
-            controls = [pick_control(i, m0, m1) for i in tiles]
-            for i, control in zip(tiles, controls):
-                pick_difference(i, control, x1[c][0], m0, m1)
-
-        control4 = pick_control(4, *chunks[1])
-        control7 = pick_control(7, *chunks[0])
-        pick_difference(4, control4, x1[1][0], *chunks[1])
-        pick_difference(7, control7, x1[0][0], *chunks[0])
+        x1.append(x_tiles("x1_1", 128, "x1_32_1", "x1_16_1"))
+        controls.append(pick_control(7))
+        pick_difference(4, x1[1][0], *chunks[1])
+        pick_difference(7, x1[0][0], *chunks[0])
         round_x(nc.scalar.copy, x1[0][0], x1[0][1], 0, 256)
-        picks(1, [5, 6, 7])
+        for i in (5, 6, 7):
+            pick_difference(i, x1[1][0], *chunks[1])
         round_x(nc.scalar.copy, x1[1][0], x1[1][1], 0, 128)
         finish(0)
-        picks(2, [4, 5])
+        x1.append(x_tiles("x1_2", 128, "x1_16_0", "x1_16_2"))
+        for i in (4, 5, 6, 7):
+            pick_difference(i, x1[2][0], *chunks[2])
         finish(1)
-        picks(2, [6, 7])
         round_x(nc.vector.tensor_copy, x1[2][0], x1[2][1], 0, 128)
         finish(2)

@@ -39,12 +39,11 @@ def tile_list_clamped_pair_features_kernel(
         nc.sync.dma_start(offs_sb[:], offs)
 
         tab_bytes = keep.tile([P, T], U8, name="tab_bytes")
-        nc.sync.dma_start(tab_bytes[112:128, :].bitcast(I32), tab_scales[0].bitcast(I32))
+        wd_bytes = keep.tile([P, H], U8, name="wd_bytes")
+        nc.scalar.dma_start(tab_bytes[112:128, :].bitcast(I32), tab_scales[0].bitcast(I32))
+        nc.scalar.dma_start(wd_bytes[112:128, :].bitcast(I32), wd_scales[0].bitcast(I32))
         nc.vector.memset(tab_bytes[0:112, :].bitcast(I32), 0)
-        nc.sync.dma_start(pos1_sb[:], pos1)
-        nc.sync.dma_start(pos2_sb[:], pos2)
-        bd_sb = keep.tile([P, 2, PACK], F32, name="bd_sb")
-        nc.sync.dma_start(bd_sb[:], bd.rearrange("(b p t) -> p b t", b=2, t=PACK))
+        nc.vector.memset(wd_bytes[0:112, :].bitcast(I32), 0)
 
         tab_sb = keep.tile([P, T], U16, name="tab_sb")
         nc.sync.dma_start(tab_sb[:].bitcast(I32), tab_words[0].bitcast(I32))
@@ -76,30 +75,34 @@ def tile_list_clamped_pair_features_kernel(
                 w0 = w0 + width
             return codes, scales
 
-        def load_scale_rows(queue, dst, src):
-            for r in range(4):
-                queue.dma_start(dst[r:P:32, :, :].bitcast(I32), src[r:16:4, :, :].bitcast(I32))
-
-        raw_a = [load_weight(wa, "a", 0, c) for c in range(2)]
+        raw_a = [load_weight(wa, "a", 0, 0)]
+        nc.sync.dma_start(pos1_sb[:], pos1)
+        nc.sync.dma_start(pos2_sb[:], pos2)
+        bd_sb = keep.tile([P, 2, PACK], F32, name="bd_sb")
+        nc.sync.dma_start(bd_sb[:], bd.rearrange("(b p t) -> p b t", b=2, t=PACK))
+        raw_a.append(load_weight(wa, "a", 0, 1))
         raw_b = [load_weight(wb, "b", 0, c) for c in range(2)]
 
-        v_scales = keep.tile([P, S], U8, name="v_scales", align_bytes=64)
-        wd_bytes = keep.tile([P, H], U8, name="wd_bytes", tag="slot_scales", align_bytes=64)
         warm = keep.tile([P, 2], F32, name="warm")
         nc.gpsimd.memset(warm[:, 0:1], 0.0)
         nc.scalar.activation(warm[:, 1:2], warm[:, 0:1], ACT.Tanh)
-        nc.gpsimd.memset(wd_bytes[:].bitcast(I32), 0)
-        nc.vector.memset(v_scales[:].bitcast(I32), 0)
-        load_scale_rows(nc.gpsimd, wd_bytes[:].rearrange("p (a n) -> p a n", a=1), wd_scales.rearrange("a q n -> q a n"))
+        planes = keep.tile([P, S + H], U8, name="planes", align_bytes=64)
+        nc.gpsimd.memset(planes[:].bitcast(I32), 0)
+        v_scales, wd_dealt = planes[:, 0:S], planes[:, S : S + H]
 
-        picked_bytes = keep.tile([P, S], U8, name="picked_bytes", tag="slot_picked")
+        picked_bytes = keep.tile([P, S], U8, name="picked_bytes")
+        staged = keep.tile([P, S + H], U8, name="staged", tag="slot_picked")
         nc.vector.tensor_copy(picked_bytes[:], tab_bytes[:].indirect(offs_sb[:]))
+        nc.vector.tensor_copy(
+            staged[:, S : S + H].rearrange("p (b t g i) -> p b g t i", b=2, t=PACK, i=16),
+            wd_bytes[:].rearrange("p (b g i t) -> p b g t i", b=2, t=PACK, i=16),
+        )
+        nc.vector.tensor_copy(staged[:, 0:S].bitcast(I32), picked_bytes[:].bitcast(I32))
         for quad in range(4):
-            nc.scalar.dma_start(
-                v_scales[32 * quad : 32 * quad + 4, :].bitcast(I32),
-                picked_bytes[112 + 4 * quad : 116 + 4 * quad, :].bitcast(I32),
+            nc.sync.dma_start(
+                planes[32 * quad : 32 * quad + 4, :].bitcast(I32),
+                staged[112 + 4 * quad : 116 + 4 * quad, :].bitcast(I32),
             )
-
         b4_sb = keep.tile([P, N // P], F32, name="b4_sb", tag="slot_picked")
         with nc.allow_non_contiguous_dma(reason="one bias value a partition"):
             nc.sync.dma_start(b4_sb[:], b4.rearrange("(c p) -> p c", p=P))
@@ -131,21 +134,15 @@ def tile_list_clamped_pair_features_kernel(
         ga, gb = grouped_tile("ga0", "slot_ga"), grouped_tile("gb0", "slot_d1")
         round_weight(nc.scalar.copy, raw_a[0], ga, 0)
         round_weight(nc.scalar.copy, raw_a[1], ga, 1)
-        round_weight(nc.vector.tensor_copy, raw_b[0], gb, 0)
+        round_weight(nc.scalar.copy, raw_b[0], gb, 0)
         qa = [quantize("wa0", flat(ga), [512])]
         round_weight(nc.vector.tensor_copy, raw_b[1], gb, 1)
-        wd_dealt = keep.tile([P, H], U8, name="wd_dealt", tag="slot_ga", align_bytes=64)
-        nc.vector.tensor_copy(
-            wd_dealt[:].rearrange("p (b t g i) -> p b g t i", b=2, t=PACK, i=16),
-            wd_bytes[:].rearrange("p (b g i t) -> p b g t i", b=2, t=PACK, i=16),
-        )
         qd = [deal_wd(raw_d, 0)]
         qb = [quantize("wb0", flat(gb), [128, 128, 256])]
 
         raw_a = [load_weight(wa, "a", 1, c) for c in range(2)]
         raw_b = [load_weight(wb, "b", 1, c) for c in range(2)]
         raw_d = load_wd(1)
-        ga, gb = grouped_tile("ga1", "slot_ga1"), grouped_tile("gb1", "slot_gb")
 
         h = [keep.tile([P, S], F32, name="h%d" % i) for i in range(H // P)]
 
@@ -168,7 +165,7 @@ def tile_list_clamped_pair_features_kernel(
             a_ps = product("ps_a", 2, qa[b], t, half)
             b_ps = product("ps_b", 3, qb[b], t, half)
             e_ps = product("ps_e", 3, qd[b], t, half)
-            a_sb = ring.tile([P, BANK], F32, name="a_sb")
+            a_sb = ring.tile([P, BANK], F32, name="a_sb", bufs=4)
             nc.scalar.copy(a_sb[:], a_ps[:])
             return a_sb, b_ps, e_ps
 
@@ -222,25 +219,34 @@ def tile_list_clamped_pair_features_kernel(
             floored0 = floor(units[0])
             if i > 0:
                 controls.append(pick_control(i - 1))
-            last = keep.tile([P, BANK], F32, name="last", tag="x1_32_1", align_bytes=64) if i == 7 else None
+            last = None
+            if i in (0, 1, 7):
+                last = keep.tile([P, BANK], F32, name="last%d" % i, tag={0: "slot_ga1", 1: "slot_gb", 7: "x1_32_1"}[i], align_bytes=64)
             floored1 = floor(units[1], last)
             ceiling(units[0], floored0, b, t, 0)
             if i > 0:
                 pick_difference(i - 1, *inline_picks(i - 1))
             ceiling(units[1], floored1, b, t, 1)
             if i == 0:
+                ga = grouped_tile("ga1", "slot_ga1")
                 round_weight(nc.scalar.copy, raw_a[0], ga, 0)
                 round_weight(nc.scalar.copy, raw_a[1], ga, 1)
             if i == 1:
+                gb = grouped_tile("gb1", "slot_gb")
                 round_weight(nc.scalar.copy, raw_b[0], gb, 0)
                 round_weight(nc.scalar.copy, raw_b[1], gb, 1)
-                qa.append(quantize("wa1", flat(ga), [512]))
                 qd.append(deal_wd(raw_d, 1))
                 w4_sb = keep.tile([P, 2, 2 * N], U8, name="w4_sb", tag="slot_d1", align_bytes=64)
                 nc.sync.dma_start(w4_sb[:].bitcast(I32), w4_words.rearrange("a p n -> p a n").bitcast(I32))
-                w4_scales_sb = keep.tile([P, 2, N], U8, name="w4_scales_sb", tag="slot_scales", align_bytes=64)
+                w4_scales_sb = keep.tile([P, 2, N], U8, name="w4_scales_sb", tag="slot_ga", align_bytes=64)
                 nc.gpsimd.memset(w4_scales_sb[:].rearrange("p a n -> p (a n)").bitcast(I32), 0)
-                load_scale_rows(nc.sync, w4_scales_sb[:], w4_scales.rearrange("a q n -> q a n"))
+                for r in range(4):
+                    nc.sync.dma_start(
+                        w4_scales_sb[r:P:32, :, :].bitcast(I32),
+                        w4_scales.rearrange("a q n -> q a n")[r:16:4, :, :].bitcast(I32),
+                    )
+            if i == 1:
+                qa.append(quantize("wa1", flat(ga), [512]))
             if i == 2:
                 qb.append(quantize("wb1", flat(gb), [512]))
             if i == 4:

from contextlib import ExitStack

import concourse.mybir as mybir

K, T, S, H, M, N = 512, 4096, 1024, 1024, 512, 384
FLOPS = 3 * 2 * K * H * S + 2 * H * N * M

F32 = mybir.dt.float32
BF16 = mybir.dt.bfloat16
I32 = mybir.dt.int32
U32 = mybir.dt.uint32
U16 = mybir.dt.uint16
U8 = mybir.dt.uint8
FP8X4 = mybir.dt.float8_e4m3fn_x4
FP4X4 = mybir.dt.float4_e2m1fn_x4
ALU = mybir.AluOpType
ACT = mybir.ActivationFunctionType

P = 128
PACK = 4
PASS = P * PACK
BANK = 512
LOAD_COLS = 256
UNIT = 128


def tile_list_clamped_pair_features_kernel(
    tc, tab_words, tab_scales, offs, pos1, pos2, wa, wb, wd_words, wd_scales, bd, w4_words, w4_scales, b4, out
):
    nc = tc.nc
    with ExitStack() as ctx:
        keep = ctx.enter_context(tc.tile_pool(name="keep", bufs=1))
        ring = ctx.enter_context(tc.tile_pool(name="ring", bufs=3))
        psum = ctx.enter_context(tc.psum_pool(name="psum", bufs=1))

        offs_sb = keep.tile([P, S // 16], U16, name="offs_sb")
        pos1_sb = keep.tile([P, M // 16], U16, name="pos1_sb")
        pos2_sb = keep.tile([P, M // 16], U16, name="pos2_sb")
        nc.sync.dma_start(offs_sb[:], offs)

        tab_bytes = keep.tile([P, T], U8, name="tab_bytes")
        wd_bytes = keep.tile([P, H], U8, name="wd_bytes")
        nc.scalar.dma_start(tab_bytes[112:128, :].bitcast(I32), tab_scales[0].bitcast(I32))
        nc.scalar.dma_start(wd_bytes[112:128, :].bitcast(I32), wd_scales[0].bitcast(I32))
        nc.vector.memset(tab_bytes[0:112, :].bitcast(I32), 0)
        nc.vector.memset(wd_bytes[0:112, :].bitcast(I32), 0)

        tab_sb = keep.tile([P, T], U16, name="tab_sb")
        nc.sync.dma_start(tab_sb[:].bitcast(I32), tab_words[0].bitcast(I32))

        def load_weight(w, which, b, c):
            raw = keep.tile([P, PACK, LOAD_COLS], F32, name="raw_%s%d%d" % (which, b, c), tag="slot_%s%d" % (which, c), align_bytes=64)
            c0 = PASS * b + LOAD_COLS * c
            nc.sync.dma_start(raw[:], w.rearrange("(p j) r -> p j r", j=PACK)[:, :, c0 : c0 + LOAD_COLS])
            return raw

        def round_weight(copy, raw, grouped, c):
            q0, nq = c * LOAD_COLS // PACK, LOAD_COLS // PACK
            copy(
                grouped[:, :, q0 : q0 + nq, :].rearrange("p t q j -> p q t j"),
                raw[:].rearrange("p j (q t) -> p q t j", t=PACK),
            )

        def quantize(name, grouped_flat, widths):
            words = grouped_flat.shape[1] // PACK
            codes = keep.tile([P, words], U32, name=name + "_codes", align_bytes=64)
            scales = keep.tile([P, words], U8, name=name + "_scales", align_bytes=64)
            w0 = 0
            for width in widths:
                nc.vector.quantize_mx(
                    out=codes[:, w0 : w0 + width].bitcast(FP8X4),
                    scales=scales[:, w0 : w0 + width],
                    in_=grouped_flat[:, PACK * w0 : PACK * (w0 + width)],
                )
                w0 = w0 + width
            return codes, scales

        raw_a = [load_weight(wa, "a", 0, 0)]
        nc.sync.dma_start(pos1_sb[:], pos1)
        nc.sync.dma_start(pos2_sb[:], pos2)
        bd_sb = keep.tile([P, 2, PACK], F32, name="bd_sb")
        nc.sync.dma_start(bd_sb[:], bd.rearrange("(b p t) -> p b t", b=2, t=PACK))
        raw_a.append(load_weight(wa, "a", 0, 1))
        raw_b = [load_weight(wb, "b", 0, c) for c in range(2)]

        warm = keep.tile([P, 2], F32, name="warm")
        nc.gpsimd.memset(warm[:, 0:1], 0.0)
        nc.scalar.activation(warm[:, 1:2], warm[:, 0:1], ACT.Tanh)
        planes = keep.tile([P, S + H], U8, name="planes", align_bytes=64)
        nc.gpsimd.memset(planes[:].bitcast(I32), 0)
        v_scales, wd_dealt = planes[:, 0:S], planes[:, S : S + H]

        picked_bytes = keep.tile([P, S], U8, name="picked_bytes")
        staged = keep.tile([P, S + H], U8, name="staged", tag="slot_picked")
        nc.vector.tensor_copy(picked_bytes[:], tab_bytes[:].indirect(offs_sb[:]))
        nc.vector.tensor_copy(
            staged[:, S : S + H].rearrange("p (b t g i) -> p b g t i", b=2, t=PACK, i=16),
            wd_bytes[:].rearrange("p (b g i t) -> p b g t i", b=2, t=PACK, i=16),
        )
        nc.vector.tensor_copy(staged[:, 0:S].bitcast(I32), picked_bytes[:].bitcast(I32))
        for quad in range(4):
            nc.sync.dma_start(
                planes[32 * quad : 32 * quad + 4, :].bitcast(I32),
                staged[112 + 4 * quad : 116 + 4 * quad, :].bitcast(I32),
            )
        b4_sb = keep.tile([P, N // P], F32, name="b4_sb", tag="slot_picked")
        with nc.allow_non_contiguous_dma(reason="one bias value a partition"):
            nc.sync.dma_start(b4_sb[:], b4.rearrange("(c p) -> p c", p=P))

        v_words = keep.tile([P, S], U16, name="v_words", align_bytes=64)
        nc.vector.tensor_copy(v_words[:], tab_sb[:].indirect(offs_sb[:]))

        def load_wd(b):
            raw = keep.tile([P, PASS], I32, name="raw_d%d" % b, tag="slot_d%d" % b, align_bytes=64)
            flat = wd_words[0].rearrange("p r i -> p (r i)")
            nc.sync.dma_start(raw[:], flat[:, PACK * PASS * b : PACK * PASS * (b + 1)].bitcast(I32))
            return raw

        def deal_wd(raw, b):
            codes = keep.tile([P, PASS], I32, name="wd_codes%d" % b, align_bytes=64)
            nc.vector.tensor_copy(
                codes[:].rearrange("p (t g i) -> p g t i", t=PACK, i=4),
                raw[:].rearrange("p (g i t) -> p g t i", t=PACK, i=4),
            )
            return codes, wd_dealt[:, PASS * b : PASS * (b + 1)]

        def grouped_tile(name, tag):
            return keep.tile([P, PACK, P, PACK], BF16, name=name, tag=tag, align_bytes=64)

        def flat(grouped):
            return grouped[:].rearrange("p t q j -> p (t q j)")

        raw_d = load_wd(0)
        ga, gb = grouped_tile("ga0", "slot_ga"), grouped_tile("gb0", "slot_d1")
        round_weight(nc.scalar.copy, raw_a[0], ga, 0)
        round_weight(nc.scalar.copy, raw_a[1], ga, 1)
        round_weight(nc.scalar.copy, raw_b[0], gb, 0)
        qa = [quantize("wa0", flat(ga), [512])]
        round_weight(nc.vector.tensor_copy, raw_b[1], gb, 1)
        qd = [deal_wd(raw_d, 0)]
        qb = [quantize("wb0", flat(gb), [128, 128, 256])]

        raw_a = [load_weight(wa, "a", 1, c) for c in range(2)]
        raw_b = [load_weight(wb, "b", 1, c) for c in range(2)]
        raw_d = load_wd(1)

        h = [keep.tile([P, S], F32, name="h%d" % i) for i in range(H // P)]

        def product(tag, bufs, operand, t, half):
            codes, scales = operand
            acc = psum.tile([P, BANK], F32, name=tag, tag=tag, bufs=bufs)
            cols = slice(BANK * half, BANK * (half + 1))
            nc.tensor.matmul_mx(
                out=acc[:],
                lhsT=codes[:, P * t : P * (t + 1)].bitcast(FP8X4),
                lhsT_scale=scales[:, P * t : P * (t + 1)],
                rhs=v_words[:, cols].bitcast(FP4X4),
                rhs_scale=v_scales[:, cols],
                start=True,
                stop=True,
            )
            return acc

        def products(b, t, half):
            a_ps = product("ps_a", 2, qa[b], t, half)
            b_ps = product("ps_b", 3, qb[b], t, half)
            e_ps = product("ps_e", 3, qd[b], t, half)
            a_sb = ring.tile([P, BANK], F32, name="a_sb", bufs=4)
            nc.scalar.copy(a_sb[:], a_ps[:])
            return a_sb, b_ps, e_ps

        def floor(unit, floored=None):
            if floored is None:
                floored = ring.tile([P, BANK], F32, name="floored")
            nc.vector.tensor_tensor(floored[:], unit[1][:], unit[0][:], ALU.max)
            return floored

        def ceiling(unit, floored, b, t, half):
            nc.vector.scalar_tensor_tensor(
                h[PACK * b + t][:, BANK * half : BANK * (half + 1)],
                unit[2][:], bd_sb[:, b, t : t + 1], floored[:], ALU.add, ALU.min,
            )

        def pick_control(i):
            control = keep.tile([P, M], F32, name="control%d" % i, tag="control%d" % (i % PACK))
            nc.vector.tensor_copy(control[:], h[i][:].indirect(pos2_sb[:]))
            return control

        def pick_difference(i, x32, m0, m1):
            nc.vector.tensor_tensor(
                x32[:, i % PACK, :], h[i][:].indirect(pos1_sb[:, m0 // 16 : m1 // 16]), controls[i][:, m0:m1], ALU.subtract
            )

        def round_x(copy, x32, x16, m0, m1):
            copy(
                x16[:, m0:m1, :].rearrange("p (g i) t -> p g t i", i=4),
                x32[:, :, m0:m1].rearrange("p t (g i) -> p g t i", i=4),
            )

        def x_tiles(name, width, tag32, tag16):
            x32 = keep.tile([P, PACK, width], F32, name=name + "_32", tag=tag32, align_bytes=64)
            x16 = keep.tile([P, width, PACK], BF16, name=name + "_16", tag=tag16, align_bytes=64)
            return x32, x16

        x0_32, x0_16 = x_tiles("x0", M, "x0_32", "x0_16")
        chunks = [(0, 256), (256, 384), (384, 512)]
        x1 = [x_tiles("x1_%d" % c, chunks[c][1] - chunks[c][0], "x1_32_%d" % c, "x1_16_%d" % c) for c in range(1)]
        controls = []

        def inline_picks(i):
            return (x0_32, 0, M) if i < PACK else (x1[0][0], chunks[0][0], chunks[0][1])

        w4_sb = None
        w4_scales_sb = None
        qx0 = None
        for i in range(H // P):
            b, t = divmod(i, PACK)
            units = [products(b, t, half) for half in range(2)]
            floored0 = floor(units[0])
            if i > 0:
                controls.append(pick_control(i - 1))
            last = None
            if i in (0, 1, 7):
                last = keep.tile([P, BANK], F32, name="last%d" % i, tag={0: "slot_ga1", 1: "slot_gb", 7: "x1_32_1"}[i], align_bytes=64)
            floored1 = floor(units[1], last)
            ceiling(units[0], floored0, b, t, 0)
            if i > 0:
                pick_difference(i - 1, *inline_picks(i - 1))
            ceiling(units[1], floored1, b, t, 1)
            if i == 0:
                ga = grouped_tile("ga1", "slot_ga1")
                round_weight(nc.scalar.copy, raw_a[0], ga, 0)
                round_weight(nc.scalar.copy, raw_a[1], ga, 1)
            if i == 1:
                gb = grouped_tile("gb1", "slot_gb")
                round_weight(nc.scalar.copy, raw_b[0], gb, 0)
                round_weight(nc.scalar.copy, raw_b[1], gb, 1)
                qd.append(deal_wd(raw_d, 1))
                w4_sb = keep.tile([P, 2, 2 * N], U8, name="w4_sb", tag="slot_d1", align_bytes=64)
                nc.sync.dma_start(w4_sb[:].bitcast(I32), w4_words.rearrange("a p n -> p a n").bitcast(I32))
                w4_scales_sb = keep.tile([P, 2, N], U8, name="w4_scales_sb", tag="slot_ga", align_bytes=64)
                nc.gpsimd.memset(w4_scales_sb[:].rearrange("p a n -> p (a n)").bitcast(I32), 0)
                for r in range(4):
                    nc.sync.dma_start(
                        w4_scales_sb[r:P:32, :, :].bitcast(I32),
                        w4_scales.rearrange("a q n -> q a n")[r:16:4, :, :].bitcast(I32),
                    )
            if i == 1:
                qa.append(quantize("wa1", flat(ga), [512]))
            if i == 2:
                qb.append(quantize("wb1", flat(gb), [512]))
            if i == 4:
                round_x(nc.scalar.copy, x0_32, x0_16, 0, 256)
                round_x(nc.scalar.copy, x0_32, x0_16, 256, 512)
            if i == 5:
                qx0 = quantize("x0", x0_16[:].rearrange("p m t -> p (m t)"), [512])

        def last_passes(acc, b, operand, c0):
            codes, scales = operand
            for n in range(N // P):
                nc.tensor.matmul_mx(
                    out=acc[:, UNIT * n : UNIT * (n + 1)],
                    lhsT=w4_sb[:, b, 2 * P * n : 2 * P * (n + 1)].bitcast(FP4X4),
                    lhsT_scale=w4_scales_sb[:, b, P * n : P * (n + 1)],
                    rhs=codes[:, c0 : c0 + UNIT].bitcast(FP8X4),
                    rhs_scale=scales[:, c0 : c0 + UNIT],
                    start=(b == 0 and n == 0),
                    stop=(b == 1 and n == N // P - 1),
                )

        y_ps = []
        for u, (tag, bufs) in enumerate([("ps_a", 2), ("ps_a", 2), ("ps_b", 3), ("ps_e", 3)]):
            acc = psum.tile([P, BANK], F32, name="y%d" % u, tag=tag, bufs=bufs)
            last_passes(acc, 0, qx0, UNIT * u)
            y_ps.append(acc)

        def finish(c):
            m0, m1 = chunks[c]
            qx = quantize("x1_%d" % c, x1[c][1][:].rearrange("p m t -> p (m t)"), [m1 - m0])
            for u in range(m0 // UNIT, m1 // UNIT):
                last_passes(y_ps[u], 1, qx, UNIT * u - m0)
                result = keep.tile([P, N // P, UNIT], F32, name="result%d" % u)
                for n in range(N // P):
                    nc.scalar.activation(
                        result[:, n, :], y_ps[u][:, UNIT * n : UNIT * (n + 1)], ACT.Tanh, bias=b4_sb[:, n : n + 1]
                    )
                    nc.sync.dma_start(out[P * n : P * (n + 1), UNIT * u : UNIT * (u + 1)], result[:, n, :])

        x1.append(x_tiles("x1_1", 128, "x1_32_1", "x1_16_1"))
        controls.append(pick_control(7))
        pick_difference(4, x1[1][0], *chunks[1])
        pick_difference(7, x1[0][0], *chunks[0])
        round_x(nc.scalar.copy, x1[0][0], x1[0][1], 0, 256)
        for i in (5, 6, 7):
            pick_difference(i, x1[1][0], *chunks[1])
        round_x(nc.scalar.copy, x1[1][0], x1[1][1], 0, 128)
        finish(0)
        x1.append(x_tiles("x1_2", 128, "x1_16_0", "x1_16_2"))
        for i in (4, 5, 6, 7):
            pick_difference(i, x1[2][0], *chunks[2])
        finish(1)
        round_x(nc.vector.tensor_copy, x1[2][0], x1[2][1], 0, 128)
        finish(2)
